import numpy as np
import ml_dtypes

BF16 = ml_dtypes.bfloat16


def bf(x):
    return np.asarray(x, np.float32).astype(BF16)


def f32(x):
    return np.asarray(x, np.float32)


def f64(x):
    return np.asarray(x).astype(np.float64)


def striped(idx):
    return np.tile(idx.reshape(-1, 16).T, (8, 1))


def rows(idx, k):
    return np.tile(idx, (k, 1))


def look(tab, idx):
    return np.take_along_axis(f64(tab), rows(idx, len(tab)), axis=1)


K, S, D, V, N, M = 512, 2048, 4, 512, 2048, 256


def setup_inputs():
    return {"tab": f32(np.random.standard_normal((K, S))), "x0": f32(np.random.standard_normal((K, V))), "w": bf(np.random.standard_normal((K, M)) / np.sqrt(K)), "offs": striped(np.random.permutation(S)[:N])}


def reference(tab, x0, w, offs):
    idx = offs[:16].T.reshape(-1)
    x = f64(x0)
    for d in range(D):
        x = np.minimum(x, look(tab, idx[d * V:(d + 1) * V]))
    y = f64(w).T @ x
    return y

@@ -1,0 +1,54 @@
+import concourse.mybir as mybir
+
+P = 128
+K, S, D, V, M = 512, 2048, 4, 512, 256
+GROUP = 16
+BLOCKS = K // P
+HALVES = M // P
+FLOPS = 2 * K * M * V
+
+F32, BF16, U16 = mybir.dt.float32, mybir.dt.bfloat16, mybir.dt.uint16
+MIN = mybir.AluOpType.min
+
+
+def tile_lookup_pool_min_none_kernel(tc, tab, x0, w, offs, out):
+    nc = tc.nc
+    with (
+        tc.tile_pool(name="held", bufs=1) as held,
+        tc.tile_pool(name="running", bufs=3) as running,
+        tc.psum_pool(name="psum", bufs=1) as psum,
+    ):
+        offsets = held.tile([P, D * V // GROUP], U16, name="offsets")
+        nc.sync.dma_start(offsets[:], offs)
+        windows, centres = [], []
+        weights = held.tile([P, BLOCKS, M], BF16, name="weights")
+        for b in range(BLOCKS):
+            rows = slice(b * P, (b + 1) * P)
+            window = held.tile([P, S], F32, name=f"window{b}")
+            centre = held.tile([P, V], F32, name=f"centre{b}")
+            nc.sync.dma_start(window[:], tab[rows, :])
+            nc.sync.dma_start(centre[:], x0[rows, :])
+            windows.append(window)
+            centres.append(centre)
+            nc.sync.dma_start(weights[:, b, :], w[rows, :])
+
+        banks = [psum.tile([P, V], F32, name=f"bank{h}") for h in range(HALVES)]
+        for b in range(BLOCKS):
+            smallest = centres[b]
+            for d in range(D):
+                piece = offsets[:, d * V // GROUP : (d + 1) * V // GROUP]
+                lower = running.tile([P, V], F32, name="lower")
+                nc.vector.tensor_tensor(lower[:], windows[b][:].indirect(piece), smallest[:], MIN)
+                smallest = lower
+            pooled = running.tile([P, V], BF16, name="pooled")
+            nc.scalar.copy(pooled[:], smallest[:])
+            for h in range(HALVES):
+                nc.tensor.matmul(
+                    banks[h][:], weights[:, b, h * P : (h + 1) * P], pooled[:],
+                    start=b == 0, stop=b == BLOCKS - 1,
+                )
+
+        for h, copy in enumerate((nc.scalar.copy, nc.vector.tensor_copy)):
+            staged = held.tile([P, V], F32, name=f"staged{h}")
+            copy(staged[:], banks[h][:])
+            nc.sync.dma_start(out[h * P : (h + 1) * P, :], staged[:])

@@ -5,6 +5,7 @@ K, S, D, V, M = 512, 2048, 4, 512, 256
 GROUP = 16
 BLOCKS = K // P
 HALVES = M // P
+QUARTER = V // 4
 FLOPS = 2 * K * M * V
 
 F32, BF16, U16 = mybir.dt.float32, mybir.dt.bfloat16, mybir.dt.uint16
@@ -15,40 +16,75 @@ def tile_lookup_pool_min_none_kernel(tc, tab, x0, w, offs, out):
     nc = tc.nc
     with (
         tc.tile_pool(name="held", bufs=1) as held,
-        tc.tile_pool(name="running", bufs=3) as running,
+        tc.tile_pool(name="running", bufs=6) as running,
         tc.psum_pool(name="psum", bufs=1) as psum,
     ):
         offsets = held.tile([P, D * V // GROUP], U16, name="offsets")
-        nc.sync.dma_start(offsets[:], offs)
-        windows, centres = [], []
+        windows = [held.tile([P, S], F32, name=f"window{b}") for b in range(BLOCKS)]
+        centres = held.tile([P, BLOCKS, V], F32, name="centres")
         weights = held.tile([P, BLOCKS, M], BF16, name="weights")
-        for b in range(BLOCKS):
-            rows = slice(b * P, (b + 1) * P)
-            window = held.tile([P, S], F32, name=f"window{b}")
-            centre = held.tile([P, V], F32, name=f"centre{b}")
-            nc.sync.dma_start(window[:], tab[rows, :])
-            nc.sync.dma_start(centre[:], x0[rows, :])
-            windows.append(window)
-            centres.append(centre)
-            nc.sync.dma_start(weights[:, b, :], w[rows, :])
+        x0_blocks = x0.rearrange("(b p) v -> p b v", p=P)
 
-        banks = [psum.tile([P, V], F32, name=f"bank{h}") for h in range(HALVES)]
-        for b in range(BLOCKS):
-            smallest = centres[b]
+        nc.sync.dma_start(windows[0][:], tab[0:P, :])
+        nc.sync.dma_start(offsets[:], offs)
+        nc.sync.dma_start(centres[:, 0, :], x0_blocks[:, 0, :])
+        nc.sync.dma_start(windows[1][:], tab[P : 2 * P, :])
+        nc.sync.dma_start(centres[:, 1:, :], x0_blocks[:, 1:, :])
+        nc.sync.dma_start(weights[:], w.rearrange("(b p) m -> p b m", p=P))
+        for b in range(2, BLOCKS):
+            nc.sync.dma_start(windows[b][:], tab[b * P : (b + 1) * P, :])
+
+        banks = [
+            [psum.tile([P, QUARTER], F32, name=f"bank{q}_{h}") for h in range(HALVES)]
+            for q in range(V // QUARTER)
+        ]
+        out_halves = out.rearrange("(h p) v -> p h v", p=P)
+
+        def pool_two_chains(b, first, width):
+            starts = (first, first + width)
+            smallest = [centres[:, b, s : s + width] for s in starts]
             for d in range(D):
-                piece = offsets[:, d * V // GROUP : (d + 1) * V // GROUP]
-                lower = running.tile([P, V], F32, name="lower")
-                nc.vector.tensor_tensor(lower[:], windows[b][:].indirect(piece), smallest[:], MIN)
-                smallest = lower
-            pooled = running.tile([P, V], BF16, name="pooled")
-            nc.scalar.copy(pooled[:], smallest[:])
-            for h in range(HALVES):
-                nc.tensor.matmul(
-                    banks[h][:], weights[:, b, h * P : (h + 1) * P], pooled[:],
-                    start=b == 0, stop=b == BLOCKS - 1,
-                )
+                for c, s in enumerate(starts):
+                    entry = d * V + s
+                    piece = offsets[:, entry // GROUP : (entry + width) // GROUP]
+                    lower = running.tile([P, width], F32, name="lower")
+                    nc.vector.tensor_tensor(lower[:], windows[b][:].indirect(piece), smallest[c], MIN)
+                    smallest[c] = lower[:]
+            return list(zip(starts, smallest))
 
-        for h, copy in enumerate((nc.scalar.copy, nc.vector.tensor_copy)):
-            staged = held.tile([P, V], F32, name=f"staged{h}")
-            copy(staged[:], banks[h][:])
-            nc.sync.dma_start(out[h * P : (h + 1) * P, :], staged[:])
+        def round_to_bf16(smallest, width, copy):
+            pooled = running.tile([P, width], BF16, name="pooled")
+            copy(pooled[:], smallest)
+            return pooled
+
+        def project(b, start, width, pooled):
+            for h in range(HALVES):
+                for j in range(0, width, QUARTER):
+                    nc.tensor.matmul(
+                        banks[(start + j) // QUARTER][h][:],
+                        weights[:, b, h * P : (h + 1) * P],
+                        pooled[:, j : j + QUARTER],
+                        start=b == 0,
+                        stop=b == BLOCKS - 1,
+                    )
+
+        def store(start, copies):
+            q = start // QUARTER
+            staged = held.tile([P, HALVES, QUARTER], F32, name=f"staged{q}")
+            for h, copy in enumerate(copies):
+                copy(staged[:, h, :], banks[q][h][:])
+            nc.sync.dma_start(out_halves[:, :, start : start + QUARTER], staged[:])
+
+        for b in range(BLOCKS - 1):
+            for start, smallest in pool_two_chains(b, 0, V // 2):
+                project(b, start, V // 2, round_to_bf16(smallest, V // 2, nc.scalar.copy))
+
+        last = BLOCKS - 1
+        for start, smallest in pool_two_chains(last, 0, QUARTER):
+            project(last, start, QUARTER, round_to_bf16(smallest, QUARTER, nc.scalar.copy))
+            store(start, (nc.scalar.copy, nc.scalar.copy))
+        chains = pool_two_chains(last, V // 2, QUARTER)
+        for (start, smallest), copy in zip(chains, (nc.scalar.copy, nc.vector.tensor_copy)):
+            project(last, start, QUARTER, round_to_bf16(smallest, QUARTER, copy))
+        for start, smallest in chains:
+            store(start, (nc.scalar.copy, nc.vector.tensor_copy))

@@ -4,19 +4,25 @@ P = 128
 K, S, D, V, M = 512, 2048, 4, 512, 256
 GROUP = 16
 BLOCKS = K // P
-HALVES = M // P
-QUARTER = V // 4
+OUT_BLOCKS = M // P
+HALF, QUARTER = V // 2, V // 4
 FLOPS = 2 * K * M * V
 
 F32, BF16, U16 = mybir.dt.float32, mybir.dt.bfloat16, mybir.dt.uint16
 MIN = mybir.AluOpType.min
+
+OUT_PIECES = (slice(0, HALF), slice(HALF, HALF + QUARTER), slice(HALF + QUARTER, V))
+
+
+def width(cols):
+    return cols.stop - cols.start
 
 
 def tile_lookup_pool_min_none_kernel(tc, tab, x0, w, offs, out):
     nc = tc.nc
     with (
         tc.tile_pool(name="held", bufs=1) as held,
-        tc.tile_pool(name="running", bufs=6) as running,
+        tc.tile_pool(name="running", bufs=32) as running,
         tc.psum_pool(name="psum", bufs=1) as psum,
     ):
         offsets = held.tile([P, D * V // GROUP], U16, name="offsets")
@@ -24,10 +30,13 @@ def tile_lookup_pool_min_none_kernel(tc, tab, x0, w, offs, out):
         centres = held.tile([P, BLOCKS, V], F32, name="centres")
         weights = held.tile([P, BLOCKS, M], BF16, name="weights")
         x0_blocks = x0.rearrange("(b p) v -> p b v", p=P)
+        out_blocks = out.rearrange("(h p) v -> p h v", p=P)
+        halves = (slice(0, HALF), slice(HALF, V))
 
         nc.sync.dma_start(windows[0][:], tab[0:P, :])
         nc.sync.dma_start(offsets[:], offs)
-        nc.sync.dma_start(centres[:, 0, :], x0_blocks[:, 0, :])
+        for half in halves:
+            nc.sync.dma_start(centres[:, 0, half], x0_blocks[:, 0, half])
         nc.sync.dma_start(windows[1][:], tab[P : 2 * P, :])
         nc.sync.dma_start(centres[:, 1:, :], x0_blocks[:, 1:, :])
         nc.sync.dma_start(weights[:], w.rearrange("(b p) m -> p b m", p=P))
@@ -35,56 +44,52 @@ def tile_lookup_pool_min_none_kernel(tc, tab, x0, w, offs, out):
             nc.sync.dma_start(windows[b][:], tab[b * P : (b + 1) * P, :])
 
         banks = [
-            [psum.tile([P, QUARTER], F32, name=f"bank{q}_{h}") for h in range(HALVES)]
-            for q in range(V // QUARTER)
+            [psum.tile([P, width(piece)], F32, name=f"bank{n}_{h}") for h in range(OUT_BLOCKS)]
+            for n, piece in enumerate(OUT_PIECES)
         ]
-        out_halves = out.rearrange("(h p) v -> p h v", p=P)
 
-        def pool_two_chains(b, first, width):
-            starts = (first, first + width)
-            smallest = [centres[:, b, s : s + width] for s in starts]
+        def pool_in_turn(chains):
+            smallest = [centres[:, b, cols] for b, cols in chains]
             for d in range(D):
-                for c, s in enumerate(starts):
-                    entry = d * V + s
-                    piece = offsets[:, entry // GROUP : (entry + width) // GROUP]
-                    lower = running.tile([P, width], F32, name="lower")
-                    nc.vector.tensor_tensor(lower[:], windows[b][:].indirect(piece), smallest[c], MIN)
+                for c, (b, cols) in enumerate(chains):
+                    entries = offsets[:, (d * V + cols.start) // GROUP : (d * V + cols.stop) // GROUP]
+                    lower = running.tile([P, width(cols)], F32, name="lower")
+                    nc.vector.tensor_tensor(lower[:], windows[b][:].indirect(entries), smallest[c], MIN)
                     smallest[c] = lower[:]
-            return list(zip(starts, smallest))
+            return smallest
 
-        def round_to_bf16(smallest, width, copy):
-            pooled = running.tile([P, width], BF16, name="pooled")
+        def project(b, cols, smallest, copy):
+            pooled = held.tile([P, width(cols)], BF16, name=f"pooled{b}_{cols.start}")
             copy(pooled[:], smallest)
-            return pooled
+            for h in range(OUT_BLOCKS):
+                for n, piece in enumerate(OUT_PIECES):
+                    if cols.start <= piece.start and piece.stop <= cols.stop:
+                        nc.tensor.matmul(
+                            banks[n][h][:],
+                            weights[:, b, h * P : (h + 1) * P],
+                            pooled[:, piece.start - cols.start : piece.stop - cols.start],
+                            start=b == 0,
+                            stop=b == BLOCKS - 1,
+                        )
 
-        def project(b, start, width, pooled):
-            for h in range(HALVES):
-                for j in range(0, width, QUARTER):
-                    nc.tensor.matmul(
-                        banks[(start + j) // QUARTER][h][:],
-                        weights[:, b, h * P : (h + 1) * P],
-                        pooled[:, j : j + QUARTER],
-                        start=b == 0,
-                        stop=b == BLOCKS - 1,
-                    )
-
-        def store(start, copies):
-            q = start // QUARTER
-            staged = held.tile([P, HALVES, QUARTER], F32, name=f"staged{q}")
+        def store(n, copies):
+            piece = OUT_PIECES[n]
+            staged = held.tile([P, OUT_BLOCKS, width(piece)], F32, name=f"staged{n}")
             for h, copy in enumerate(copies):
-                copy(staged[:, h, :], banks[q][h][:])
-            nc.sync.dma_start(out_halves[:, :, start : start + QUARTER], staged[:])
-
-        for b in range(BLOCKS - 1):
-            for start, smallest in pool_two_chains(b, 0, V // 2):
-                project(b, start, V // 2, round_to_bf16(smallest, V // 2, nc.scalar.copy))
+                copy(staged[:, h, :], banks[n][h][:])
+            nc.sync.dma_start(out_blocks[:, :, piece], staged[:])
 
         last = BLOCKS - 1
-        for start, smallest in pool_two_chains(last, 0, QUARTER):
-            project(last, start, QUARTER, round_to_bf16(smallest, QUARTER, nc.scalar.copy))
-            store(start, (nc.scalar.copy, nc.scalar.copy))
-        chains = pool_two_chains(last, V // 2, QUARTER)
-        for (start, smallest), copy in zip(chains, (nc.scalar.copy, nc.vector.tensor_copy)):
-            project(last, start, QUARTER, round_to_bf16(smallest, QUARTER, copy))
-        for start, smallest in chains:
-            store(start, (nc.scalar.copy, nc.vector.tensor_copy))
+        pairs = [[(b, half) for half in halves] for b in range(last - 1)]
+        pairs.append([(last - 1, slice(0, V)), (last, OUT_PIECES[0])])
+        for chains in pairs:
+            for (b, cols), smallest in zip(chains, pool_in_turn(chains)):
+                project(b, cols, smallest, nc.scalar.copy)
+        store(0, (nc.scalar.copy, nc.scalar.copy))
+
+        chains = [(last, piece) for piece in OUT_PIECES[1:]]
+        copies = (nc.scalar.copy, nc.vector.tensor_copy)
+        for (b, cols), smallest in zip(chains, pool_in_turn(chains)):
+            project(b, cols, smallest, nc.vector.tensor_copy)
+        for n in (1, 2):
+            store(n, copies)

import concourse.mybir as mybir

P = 128
K, S, D, V, M = 512, 2048, 4, 512, 256
GROUP = 16
BLOCKS = K // P
OUT_BLOCKS = M // P
HALF, QUARTER = V // 2, V // 4
FLOPS = 2 * K * M * V

F32, BF16, U16 = mybir.dt.float32, mybir.dt.bfloat16, mybir.dt.uint16
MIN = mybir.AluOpType.min

OUT_PIECES = (slice(0, HALF), slice(HALF, HALF + QUARTER), slice(HALF + QUARTER, V))


def width(cols):
    return cols.stop - cols.start


def tile_lookup_pool_min_none_kernel(tc, tab, x0, w, offs, out):
    nc = tc.nc
    with (
        tc.tile_pool(name="held", bufs=1) as held,
        tc.tile_pool(name="running", bufs=32) as running,
        tc.psum_pool(name="psum", bufs=1) as psum,
    ):
        offsets = held.tile([P, D * V // GROUP], U16, name="offsets")
        windows = [held.tile([P, S], F32, name=f"window{b}") for b in range(BLOCKS)]
        centres = held.tile([P, BLOCKS, V], F32, name="centres")
        weights = held.tile([P, BLOCKS, M], BF16, name="weights")
        x0_blocks = x0.rearrange("(b p) v -> p b v", p=P)
        out_blocks = out.rearrange("(h p) v -> p h v", p=P)
        halves = (slice(0, HALF), slice(HALF, V))

        nc.sync.dma_start(windows[0][:], tab[0:P, :])
        nc.sync.dma_start(offsets[:], offs)
        for half in halves:
            nc.sync.dma_start(centres[:, 0, half], x0_blocks[:, 0, half])
        nc.sync.dma_start(windows[1][:], tab[P : 2 * P, :])
        nc.sync.dma_start(centres[:, 1:, :], x0_blocks[:, 1:, :])
        nc.sync.dma_start(weights[:], w.rearrange("(b p) m -> p b m", p=P))
        for b in range(2, BLOCKS):
            nc.sync.dma_start(windows[b][:], tab[b * P : (b + 1) * P, :])

        banks = [
            [psum.tile([P, width(piece)], F32, name=f"bank{n}_{h}") for h in range(OUT_BLOCKS)]
            for n, piece in enumerate(OUT_PIECES)
        ]

        def pool_in_turn(chains):
            smallest = [centres[:, b, cols] for b, cols in chains]
            for d in range(D):
                for c, (b, cols) in enumerate(chains):
                    entries = offsets[:, (d * V + cols.start) // GROUP : (d * V + cols.stop) // GROUP]
                    lower = running.tile([P, width(cols)], F32, name="lower")
                    nc.vector.tensor_tensor(lower[:], windows[b][:].indirect(entries), smallest[c], MIN)
                    smallest[c] = lower[:]
            return smallest

        def project(b, cols, smallest, copy):
            pooled = held.tile([P, width(cols)], BF16, name=f"pooled{b}_{cols.start}")
            copy(pooled[:], smallest)
            for h in range(OUT_BLOCKS):
                for n, piece in enumerate(OUT_PIECES):
                    if cols.start <= piece.start and piece.stop <= cols.stop:
                        nc.tensor.matmul(
                            banks[n][h][:],
                            weights[:, b, h * P : (h + 1) * P],
                            pooled[:, piece.start - cols.start : piece.stop - cols.start],
                            start=b == 0,
                            stop=b == BLOCKS - 1,
                        )

        def store(n, copies):
            piece = OUT_PIECES[n]
            staged = held.tile([P, OUT_BLOCKS, width(piece)], F32, name=f"staged{n}")
            for h, copy in enumerate(copies):
                copy(staged[:, h, :], banks[n][h][:])
            nc.sync.dma_start(out_blocks[:, :, piece], staged[:])

        last = BLOCKS - 1
        pairs = [[(b, half) for half in halves] for b in range(last - 1)]
        pairs.append([(last - 1, slice(0, V)), (last, OUT_PIECES[0])])
        for chains in pairs:
            for (b, cols), smallest in zip(chains, pool_in_turn(chains)):
                project(b, cols, smallest, nc.scalar.copy)
        store(0, (nc.scalar.copy, nc.scalar.copy))

        chains = [(last, piece) for piece in OUT_PIECES[1:]]
        copies = (nc.scalar.copy, nc.vector.tensor_copy)
        for (b, cols), smallest in zip(chains, pool_in_turn(chains)):
            project(b, cols, smallest, nc.vector.tensor_copy)
        for n in (1, 2):
            store(n, copies)
